import numpy as np
import ml_dtypes


def mxq(x, axis, fmt="e4m3"):
    dtype, down = {"e4m3": (ml_dtypes.float8_e4m3fn, 7), "e5m2": (ml_dtypes.float8_e5m2, 14)}[fmt]
    v = np.moveaxis(np.asarray(x, np.float32).astype(ml_dtypes.bfloat16).astype(np.float64), axis, -1)
    blocks = v.reshape(v.shape[:-1] + (-1, 32))
    amax = np.abs(blocks).max(-1, keepdims=True)
    byte = np.maximum(np.where(amax > 0, np.frexp(amax)[1] - 1 + 127, 0) - down, 1)
    scale = np.exp2(byte - 127.0)
    codes = (blocks / scale).astype(np.float32).astype(dtype).astype(np.float64)
    return np.moveaxis((codes * scale).reshape(v.shape), -1, axis)


WIDE = False


def mx_kscale(k):
    if not WIDE:
        return np.ones(k)
    levels = np.array([10, -10, 5, -5, 0])
    if k % 512:
        return np.exp2(np.random.permutation(np.resize(levels, k // 32))).repeat(32)
    a = np.empty((k // 512, 16))
    for p in range(k // 512):
        a[p, :8] = np.random.permutation(np.resize(levels, 8))
        for g in range(8):
            far = levels[np.abs(levels - a[p, g]) >= 10]
            a[p, g + 8] = far[np.random.randint(len(far))]
    return np.exp2(a.ravel()).repeat(32)


def f64(x):
    return np.asarray(x).astype(np.float64)


def striped(idx):
    return np.tile(np.asarray(idx).reshape(-1, 16).T, (8, 1)).astype(np.uint16)


def unstriped(offs):
    return offs[:16].T.reshape(-1).astype(np.int64)


E2M1 = np.array([0.0, 0.5, 1.0, 1.5, 2.0, 3.0, 4.0, 6.0, -0.0, -0.5, -1.0, -1.5, -2.0, -3.0, -4.0, -6.0])


def pack_weight(w, fmt):
    k, n = w.shape
    w = f64(np.asarray(w, np.float32).astype(ml_dtypes.bfloat16)).reshape(k // 32, 32, n)
    amax = np.abs(w).max(1)
    if fmt == "e4m3":
        byte = np.frexp(amax)[1] - 1 + 127 - 7
    else:
        mant, ex = np.frexp(amax / 6.0)
        byte = np.where(mant > 0.5, ex, ex - 1) + 127
    byte = np.clip(np.where(amax > 0, byte, 1), 1, 254)
    scaled = (w * np.exp2(127.0 - byte)[:, None, :]).reshape(k, n).astype(np.float32)
    by_word = np.ascontiguousarray(scaled.reshape(k // 512, 128, 4, n).transpose(0, 1, 3, 2))
    if fmt == "e4m3":
        words = by_word.astype(ml_dtypes.float8_e4m3fn).view(np.uint8)
    else:
        c = by_word.astype(ml_dtypes.float4_e2m1fn).view(np.uint8) & 0xF
        words = (c[..., 0::2] | (c[..., 1::2] << 4)).reshape(k // 512, 128, 2 * n)
    return np.ascontiguousarray(words), np.ascontiguousarray(byte.astype(np.uint8).reshape(k // 512, 16, n))


def unpack_weight(words, scales, fmt):
    g, _, n = scales.shape
    words = np.ascontiguousarray(words).reshape(g, 128, n, -1)
    if fmt == "e4m3":
        vals = words.view(ml_dtypes.float8_e4m3fn).astype(np.float64)
    else:
        nib = np.empty((g, 128, n, 4), np.uint8)
        nib[..., 0::2] = words & 0xF
        nib[..., 1::2] = words >> 4
        vals = E2M1[nib]
    vals = vals * np.repeat(np.exp2(scales.astype(np.float64) - 127.0), 8, axis=1)[..., None]
    return vals.transpose(0, 1, 3, 2).reshape(g * 512, n)


def sigmoid(v):
    return 1.0 / (1.0 + np.exp(-v))


def bf(x):
    return np.asarray(x, np.float32).astype(ml_dtypes.bfloat16)


def planes(Y):
    r, m = Y.shape
    b = f64(bf(Y)).reshape(r // 32, 32, m)
    amax = np.abs(b).max(1)
    byte = np.clip(np.where(amax > 0, np.frexp(amax)[1] - 1 + 127 - 7, 1), 1, 254)
    codes = (b * np.exp2(127.0 - byte)[:, None, :]).reshape(r, m).astype(np.float32).astype(ml_dtypes.float8_e4m3fn).view(np.uint8)
    words = codes.reshape(r // 512, 128, 4, m).transpose(0, 1, 3, 2)
    return np.ascontiguousarray(words), np.ascontiguousarray(byte.astype(np.uint8).reshape(r // 512, 16, m))


K, T, I, G, E = 512, 2048, 1024, 128, 512


def setup_inputs():
    n = np.random.standard_normal
    idx = np.random.permutation(T)[:I]
    fk = mx_kscale(K)
    nodep = pack_weight(n((K, T)) / fk[:, None], "e4m3")
    return {
        "node_words": nodep[0],
        "node_scales": nodep[1],
        "wg": (n((K, E)) * 1 / np.sqrt(K) * fk[:, None]).astype(np.float32),
        "wv": (n((K, E)) * 1 / np.sqrt(K) * fk[:, None]).astype(np.float32),
        "bg": (0.5 * n((E, 1))).astype(np.float32),
        "offs": striped(idx),
    }


def reference(node_words, node_scales, wg, wv, bg, offs):
    idx = unstriped(offs)
    nodeu = unpack_weight(node_words, node_scales, "e4m3")
    wgq = mxq(f64(wg), 0, "e4m3")
    nodeidxg = nodeu[:, idx]
    z = wgq.T @ nodeidxg
    wvq = mxq(f64(wv), 0, "e4m3")
    v = wvq.T @ nodeidxg
    x = sigmoid(z + f64(bg)) * np.tanh(v)
    y = x.reshape(E, G, I // G).sum(axis=2)
    words, scales = planes(y)
    return y, words, scales

@@ -1,0 +1,200 @@
+from contextlib import ExitStack
+
+import concourse.mybir as mybir
+from concourse.masks import make_identity
+
+K, T, I, G, E = 512, 2048, 1024, 128, 512
+FLOPS = 2 * 2 * K * E * I
+
+F32 = mybir.dt.float32
+BF16 = mybir.dt.bfloat16
+I32 = mybir.dt.int32
+U32 = mybir.dt.uint32
+U16 = mybir.dt.uint16
+U8 = mybir.dt.uint8
+FP8X4 = mybir.dt.float8_e4m3fn_x4
+ACT = mybir.ActivationFunctionType
+ALU = mybir.AluOpType
+
+P = 128
+PACK = 4
+J = I // G
+TILES = E // P
+BANK = 512
+
+
+def tile_attend_gatedreadout_pl_kernel(tc, node_words, node_scales, wg, wv, bg, offs, out_0, out_1, out_2):
+    nc = tc.nc
+    with ExitStack() as ctx:
+        keep = ctx.enter_context(tc.tile_pool(name="keep", bufs=1))
+        work = ctx.enter_context(tc.tile_pool(name="work", bufs=2))
+        acc_pool = ctx.enter_context(tc.psum_pool(name="acc", bufs=6))
+        sum_pool = ctx.enter_context(tc.psum_pool(name="sums", bufs=1))
+
+        offsets = keep.tile([P, I // 16], U16, name="offsets")
+        nc.sync.dma_start(offsets[:], offs)
+
+        def load_weight(w, name, m0, m1):
+            raw = keep.tile([P, PACK, (m1 - m0) * P], F32, name=name)
+            nc.sync.dma_start(raw[:], w[:, m0 * P : m1 * P].rearrange("(p j) c -> p j c", j=PACK))
+            return raw
+
+        scale_pool = keep.tile([P, T], U8, name="scale_pool", align_bytes=64)
+        nc.vector.memset(scale_pool[:].bitcast(I32), 0)
+        bias_rows = keep.tile([P, P], F32, name="bias_rows")
+        nc.gpsimd.memset(bias_rows[:], 0.0)
+        ident = keep.tile([P, P], F32, name="ident")
+        make_identity(nc, ident[:])
+
+        spans = ((0, 1), (1, 2), (2, 4))
+        raws = {}
+        raws[0, 0] = load_weight(wg, "raw_g0", *spans[0])
+        for q in range(4):
+            nc.sync.dma_start(
+                scale_pool[32 * q : 32 * q + 4, :].bitcast(I32),
+                node_scales[0, 4 * q : 4 * q + 4, :].bitcast(I32),
+            )
+        nc.sync.dma_start(bias_rows[0:TILES, :], bg.rearrange("(m p) o -> m (p o)", p=P))
+        word_pool = keep.tile([P, T], I32, name="word_pool", align_bytes=64)
+        nc.sync.dma_start(word_pool[:], node_words[0].rearrange("p n t -> p (n t)").bitcast(I32))
+        raws[1, 0] = load_weight(wv, "raw_v0", *spans[0])
+        for s in (1, 2):
+            raws[0, s] = load_weight(wg, "raw_g%d" % s, *spans[s])
+            raws[1, s] = load_weight(wv, "raw_v%d" % s, *spans[s])
+
+        bias_t = acc_pool.tile([P, P], F32, name="bias_t", tag="acc")
+        nc.tensor.transpose(bias_t[:], bias_rows[:], ident[:])
+        half_bias = keep.tile([P, TILES], F32, name="half_bias")
+        nc.scalar.activation(half_bias[:], bias_t[:, 0:TILES], ACT.Copy, scale=0.5)
+
+        codes = {}
+        planes = {}
+
+        def round_weight(which, s):
+            raw = raws[which, s]
+            width = raw.shape[2]
+            tag = "late" if (which, s) == (1, 2) else "grouped%d_%d" % (which, s)
+            grouped = keep.tile([P, width * PACK], BF16, name="grouped", tag=tag, align_bytes=64)
+            dst = grouped[:].rearrange("p (c i j) -> p c j i", i=4, j=PACK)
+            src = raw[:].rearrange("p j (c i) -> p c j i", i=4)
+            if s == 0:
+                nc.scalar.activation(dst, src, ACT.Copy)
+            else:
+                nc.vector.tensor_copy(dst, src)
+            return grouped
+
+        def quantise_weight(which, s, grouped):
+            m0, m1 = spans[s]
+            width = (m1 - m0) * P
+            code = keep.tile([P, width], U32, name="wcode%d_%d" % (which, s), align_bytes=64)
+            plane = keep.tile([P, width], U8, name="wplane%d_%d" % (which, s), align_bytes=64)
+            nc.vector.quantize_mx(out=code[:].bitcast(FP8X4), scales=plane[:], in_=grouped[:])
+            for m in range(m0, m1):
+                codes[which, m] = code[:, (m - m0) * P : (m - m0 + 1) * P]
+                planes[which, m] = plane[:, (m - m0) * P : (m - m0 + 1) * P]
+
+        half = I // 2
+        quarter = I // 4
+        node_plane = [keep.tile([P, half], U8, name="nplane%d" % h, align_bytes=64) for h in range(2)]
+        node_code = [keep.tile([P, half], U32, name="ncode%d" % h, align_bytes=64) for h in range(2)]
+        quantise_weight(0, 0, round_weight(0, 0))
+        for h in range(2):
+            nc.vector.tensor_copy(node_plane[h][:], scale_pool[:].indirect(offsets[:, h * 32 : (h + 1) * 32]))
+        for s in range(4):
+            nc.vector.tensor_copy(
+                node_code[s // 2][:, (s % 2) * quarter : (s % 2 + 1) * quarter],
+                word_pool[:].bitcast(U32).indirect(offsets[:, s * 16 : (s + 1) * 16]),
+            )
+        quantise_weight(1, 0, round_weight(1, 0))
+        for s in (1, 2):
+            pair = [round_weight(which, s) for which in range(2)]
+            for which in range(2):
+                quantise_weight(which, s, pair[which])
+
+        sums_a = sum_pool.tile([P, TILES - 1, P], F32, name="sums_a")
+        sums_b = sum_pool.tile([P, P], F32, name="sums_b")
+        acts = {}
+
+        def project(which, m, h, width):
+            acc = acc_pool.tile([P, BANK], F32, name="acc", tag="acc")
+            for c in range(0, BANK, width):
+                nc.tensor.matmul_mx(
+                    out=acc[:, c : c + width],
+                    lhsT=codes[which, m].bitcast(FP8X4),
+                    lhsT_scale=planes[which, m],
+                    rhs=node_code[h][:, c : c + width].bitcast(FP8X4),
+                    rhs_scale=node_plane[h][:, c : c + width],
+                    start=True,
+                    stop=True,
+                )
+            return acc
+
+        def activate(which, m, h, acc, g0, g1, j0, j1):
+            src = acc[:].rearrange("p (g j) -> p j g", j=J)[:, j0:j1, g0:g1]
+            dst = acts[which, m][:, j0:j1, 64 * h + g0 : 64 * h + g1]
+            if which == 0:
+                nc.scalar.activation(dst, src, ACT.Tanh, bias=half_bias[:, m : m + 1], scale=0.5)
+            else:
+                nc.scalar.activation(dst, src, ACT.Tanh)
+
+        def gate(m, j0, j1):
+            tag = "late" if m == 0 else "prod%d_%d" % (m, j0)
+            prod = keep.tile([P, j1 - j0, P], F32, name="prod", tag=tag, align_bytes=64)
+            nc.vector.scalar_tensor_tensor(
+                prod[:], acts[0, m][:, j0:j1, :], 1.0, acts[1, m][:, j0:j1, :], ALU.add, ALU.mult
+            )
+            target = sums_b[:] if m == TILES - 1 else sums_a[:, m, :]
+            for j in range(j0, j1):
+                nc.tensor.matmul(target, prod[:, j - j0, :], ident[:], start=(j == 0), stop=(j == J - 1), is_transpose=True)
+
+        def front(m):
+            for which in range(2):
+                acts[which, m] = work.tile([P, J, P], F32, name="act%d" % which, tag="act%d" % which, bufs=TILES)
+            if m == 0:
+                for which in range(2):
+                    for h in range(2):
+                        acc = project(which, m, h, quarter)
+                        activate(which, m, h, acc, 0, 32, 0, J)
+                        activate(which, m, h, acc, 32, 64, 0, J)
+            elif m < TILES - 1:
+                for which in range(2):
+                    for h in range(2):
+                        activate(which, m, h, project(which, m, h, BANK), 0, 64, 0, J)
+            else:
+                for h in range(2):
+                    activate(0, m, h, project(0, m, h, BANK), 0, 64, 0, J)
+                accs = [project(1, m, h, BANK) for h in range(2)]
+                for j0, j1 in ((0, 4), (4, 6), (6, 8)):
+                    for h in range(2):
+                        activate(1, m, h, accs[h], 0, 64, j0, j1)
+
+        front(0)
+        for m in range(1, TILES):
+            front(m)
+            gate(m - 1, 0, J)
+        by_graph = keep.tile([P, PACK, P], F32, name="by_graph")
+        nc.scalar.activation(
+            by_graph[:, :, 0:96], sums_a[:].rearrange("g m (q t) -> g t (m q)", t=PACK), ACT.Copy, scale=0.5
+        )
+        for j0, j1 in ((0, 4), (4, 6), (6, 8)):
+            gate(TILES - 1, j0, j1)
+        nc.scalar.activation(by_graph[:, :, 96:128], sums_b[:].rearrange("g (q t) -> g t q", t=PACK), ACT.Copy, scale=0.5)
+
+        result = acc_pool.tile([P, PACK, P], F32, name="result", tag="acc")
+        for t in range(PACK):
+            nc.tensor.transpose(result[:, t, :], by_graph[:, t, :], ident[:])
+
+        rounded = keep.tile([P, G * PACK], BF16, name="rounded", align_bytes=64)
+        nc.vector.tensor_copy(rounded[:].rearrange("p (g t) -> p g t", t=PACK), result[:].rearrange("p t g -> p g t"))
+        y_code = keep.tile([P, G], U32, name="y_code", align_bytes=64)
+        y_plane = keep.tile([P, G], U8, name="y_plane", align_bytes=64)
+        nc.vector.quantize_mx(out=y_code[:].bitcast(FP8X4), scales=y_plane[:], in_=rounded[:])
+        y_rows = keep.tile([P, PACK, G], F32, name="y_rows")
+        nc.scalar.copy(y_rows[:], result[:])
+        nc.scalar.dma_start(out_0.rearrange("(p t) g -> p t g", t=PACK), y_rows[:])
+        nc.sync.dma_start(out_1[0].rearrange("p g t -> p (g t)").bitcast(I32), y_code[:].bitcast(I32))
+        for q in range(4):
+            engine = nc.sync if q % 2 == 0 else nc.scalar
+            engine.dma_start(
+                out_2[0, 4 * q : 4 * q + 4, :].bitcast(I32), y_plane[32 * q : 32 * q + 4, :].bitcast(I32)
+            )

@@ -50,11 +50,12 @@ def tile_attend_gatedreadout_pl_kernel(tc, node_words, node_scales, wg, wv, bg, 
         raws = {}
         raws[0, 0] = load_weight(wg, "raw_g0", *spans[0])
         for q in range(4):
-            nc.sync.dma_start(
+            engine = nc.sync if q < 2 else nc.scalar
+            engine.dma_start(
                 scale_pool[32 * q : 32 * q + 4, :].bitcast(I32),
                 node_scales[0, 4 * q : 4 * q + 4, :].bitcast(I32),
             )
-        nc.sync.dma_start(bias_rows[0:TILES, :], bg.rearrange("(m p) o -> m (p o)", p=P))
+        nc.scalar.dma_start(bias_rows[0:TILES, :], bg.rearrange("(m p) o -> m (p o)", p=P))
         word_pool = keep.tile([P, T], I32, name="word_pool", align_bytes=64)
         nc.sync.dma_start(word_pool[:], node_words[0].rearrange("p n t -> p (n t)").bitcast(I32))
         raws[1, 0] = load_weight(wv, "raw_v0", *spans[0])
@@ -130,8 +131,8 @@ def tile_attend_gatedreadout_pl_kernel(tc, node_words, node_scales, wg, wv, bg, 
             return acc
 
         def activate(which, m, h, acc, g0, g1, j0, j1):
-            src = acc[:].rearrange("p (g j) -> p j g", j=J)[:, j0:j1, g0:g1]
-            dst = acts[which, m][:, j0:j1, 64 * h + g0 : 64 * h + g1]
+            src = acc[:, g0 * J : g1 * J].rearrange("p (b i j) -> p b j i", i=4, j=J)[:, :, j0:j1, :]
+            dst = acts[which, m][:, j0:j1, 64 * h + g0 : 64 * h + g1].rearrange("p j (b i) -> p b j i", i=4)
             if which == 0:
                 nc.scalar.activation(dst, src, ACT.Tanh, bias=half_bias[:, m : m + 1], scale=0.5)
             else:
@@ -174,15 +175,26 @@ def tile_attend_gatedreadout_pl_kernel(tc, node_words, node_scales, wg, wv, bg, 
             gate(m - 1, 0, J)
         by_graph = keep.tile([P, PACK, P], F32, name="by_graph")
         nc.scalar.activation(
-            by_graph[:, :, 0:96], sums_a[:].rearrange("g m (q t) -> g t (m q)", t=PACK), ACT.Copy, scale=0.5
+            by_graph[:, :, 0:96].rearrange("g t (b i) -> g b t i", i=4),
+            sums_a[:].rearrange("g m (b i t) -> g (m b) t i", i=4, t=PACK),
+            ACT.Copy,
+            scale=0.5,
         )
         for j0, j1 in ((0, 4), (4, 6), (6, 8)):
             gate(TILES - 1, j0, j1)
-        nc.scalar.activation(by_graph[:, :, 96:128], sums_b[:].rearrange("g (q t) -> g t q", t=PACK), ACT.Copy, scale=0.5)
+        nc.scalar.activation(
+            by_graph[:, :, 96:128].rearrange("g t (b i) -> g b t i", i=4),
+            sums_b[:].rearrange("g (b i t) -> g b t i", i=4, t=PACK),
+            ACT.Copy,
+            scale=0.5,
+        )
 
         result = acc_pool.tile([P, PACK, P], F32, name="result", tag="acc")
         for t in range(PACK):
             nc.tensor.transpose(result[:, t, :], by_graph[:, t, :], ident[:])
+        result2 = acc_pool.tile([P, PACK, P], F32, name="result2", tag="acc")
+        for t in range(PACK):
+            nc.tensor.transpose(result2[:, t, :], by_graph[:, t, :], ident[:])
 
         rounded = keep.tile([P, G * PACK], BF16, name="rounded", align_bytes=64)
         nc.vector.tensor_copy(rounded[:].rearrange("p (g t) -> p g t", t=PACK), result[:].rearrange("p t g -> p g t"))
@@ -190,7 +202,7 @@ def tile_attend_gatedreadout_pl_kernel(tc, node_words, node_scales, wg, wv, bg, 
         y_plane = keep.tile([P, G], U8, name="y_plane", align_bytes=64)
         nc.vector.quantize_mx(out=y_code[:].bitcast(FP8X4), scales=y_plane[:], in_=rounded[:])
         y_rows = keep.tile([P, PACK, G], F32, name="y_rows")
-        nc.scalar.copy(y_rows[:], result[:])
+        nc.scalar.copy(y_rows[:], result2[:])
         nc.scalar.dma_start(out_0.rearrange("(p t) g -> p t g", t=PACK), y_rows[:])
         nc.sync.dma_start(out_1[0].rearrange("p g t -> p (g t)").bitcast(I32), y_code[:].bitcast(I32))
         for q in range(4):

@@ -15,90 +15,114 @@ U8 = mybir.dt.uint8
 FP8X4 = mybir.dt.float8_e4m3fn_x4
 ACT = mybir.ActivationFunctionType
 ALU = mybir.AluOpType
+AXIS = mybir.AxisListType
 
 P = 128
 PACK = 4
 J = I // G
 TILES = E // P
-BANK = 512
+LAST = TILES - 1
+CHUNKS = ((0, 44), (44, 88), (88, 128))
 
 
 def tile_attend_gatedreadout_pl_kernel(tc, node_words, node_scales, wg, wv, bg, offs, out_0, out_1, out_2):
     nc = tc.nc
     with ExitStack() as ctx:
         keep = ctx.enter_context(tc.tile_pool(name="keep", bufs=1))
-        work = ctx.enter_context(tc.tile_pool(name="work", bufs=2))
-        acc_pool = ctx.enter_context(tc.psum_pool(name="acc", bufs=6))
+        acc_pool = ctx.enter_context(tc.psum_pool(name="acc", bufs=7))
         sum_pool = ctx.enter_context(tc.psum_pool(name="sums", bufs=1))
 
         offsets = keep.tile([P, I // 16], U16, name="offsets")
         nc.sync.dma_start(offsets[:], offs)
 
-        def load_weight(w, name, m0, m1):
-            raw = keep.tile([P, PACK, (m1 - m0) * P], F32, name=name)
-            nc.sync.dma_start(raw[:], w[:, m0 * P : m1 * P].rearrange("(p j) c -> p j c", j=PACK))
-            return raw
+        weights = (wg, wv)
+        raws = [keep.tile([P, PACK, E], F32, name="raw%d" % which) for which in range(2)]
+
+        def load_weight(which, chunk):
+            c0, c1 = CHUNKS[chunk][0] * PACK, CHUNKS[chunk][1] * PACK
+            nc.sync.dma_start(
+                raws[which][:, :, c0:c1], weights[which][:, c0:c1].rearrange("(p j) c -> p j c", j=PACK)
+            )
 
         scale_pool = keep.tile([P, T], U8, name="scale_pool", align_bytes=64)
         nc.vector.memset(scale_pool[:].bitcast(I32), 0)
-        bias_rows = keep.tile([P, P], F32, name="bias_rows")
-        nc.gpsimd.memset(bias_rows[:], 0.0)
+        bias_row = keep.tile([P, E], F32, name="bias_row")
+        nc.gpsimd.memset(bias_row[:], 0.0)
         ident = keep.tile([P, P], F32, name="ident")
         make_identity(nc, ident[:])
 
-        spans = ((0, 1), (1, 2), (2, 4))
-        raws = {}
-        raws[0, 0] = load_weight(wg, "raw_g0", *spans[0])
+        load_weight(0, 0)
         for q in range(4):
             engine = nc.sync if q < 2 else nc.scalar
             engine.dma_start(
                 scale_pool[32 * q : 32 * q + 4, :].bitcast(I32),
                 node_scales[0, 4 * q : 4 * q + 4, :].bitcast(I32),
             )
-        nc.scalar.dma_start(bias_rows[0:TILES, :], bg.rearrange("(m p) o -> m (p o)", p=P))
+        load_weight(1, 0)
+        nc.sync.dma_start(bias_row[0:1, :], bg.rearrange("e o -> o e"))
         word_pool = keep.tile([P, T], I32, name="word_pool", align_bytes=64)
         nc.sync.dma_start(word_pool[:], node_words[0].rearrange("p n t -> p (n t)").bitcast(I32))
-        raws[1, 0] = load_weight(wv, "raw_v0", *spans[0])
-        for s in (1, 2):
-            raws[0, s] = load_weight(wg, "raw_g%d" % s, *spans[s])
-            raws[1, s] = load_weight(wv, "raw_v%d" % s, *spans[s])
+        for chunk in (1, 2):
+            for which in range(2):
+                load_weight(which, chunk)
 
-        bias_t = acc_pool.tile([P, P], F32, name="bias_t", tag="acc")
-        nc.tensor.transpose(bias_t[:], bias_rows[:], ident[:])
-        half_bias = keep.tile([P, TILES], F32, name="half_bias")
-        nc.scalar.activation(half_bias[:], bias_t[:, 0:TILES], ACT.Copy, scale=0.5)
-
+        grouped = [
+            keep.tile([P, LAST * P * PACK], BF16, name="grouped", tag="grouped%d" % which, align_bytes=64)
+            for which in range(2)
+        ]
+        grouped_last = keep.tile([P, 2, P * PACK], BF16, name="grouped_last", align_bytes=64)
         codes = {}
         planes = {}
 
-        def round_weight(which, s):
-            raw = raws[which, s]
-            width = raw.shape[2]
-            tag = "late" if (which, s) == (1, 2) else "grouped%d_%d" % (which, s)
-            grouped = keep.tile([P, width * PACK], BF16, name="grouped", tag=tag, align_bytes=64)
-            dst = grouped[:].rearrange("p (c i j) -> p c j i", i=4, j=PACK)
-            src = raw[:].rearrange("p j (c i) -> p c j i", i=4)
-            if s == 0:
+        def round_chunk(which, chunk):
+            l0, l1 = CHUNKS[chunk]
+            dst = grouped[which][:].rearrange("p (l t j) -> p l j t", t=LAST, j=PACK)[:, l0:l1, :, :]
+            src = raws[which][:].rearrange("p j (l t) -> p l j t", t=PACK)[:, l0:l1, :, 0:LAST]
+            if chunk == 0:
                 nc.scalar.activation(dst, src, ACT.Copy)
             else:
                 nc.vector.tensor_copy(dst, src)
-            return grouped
 
-        def quantise_weight(which, s, grouped):
-            m0, m1 = spans[s]
-            width = (m1 - m0) * P
-            code = keep.tile([P, width], U32, name="wcode%d_%d" % (which, s), align_bytes=64)
-            plane = keep.tile([P, width], U8, name="wplane%d_%d" % (which, s), align_bytes=64)
-            nc.vector.quantize_mx(out=code[:].bitcast(FP8X4), scales=plane[:], in_=grouped[:])
-            for m in range(m0, m1):
-                codes[which, m] = code[:, (m - m0) * P : (m - m0 + 1) * P]
-                planes[which, m] = plane[:, (m - m0) * P : (m - m0 + 1) * P]
+        def round_last(which, l0, l1, on_scalar):
+            dst = grouped_last[:, which, :].rearrange("p (l j) -> p l j", j=PACK)[:, l0:l1, :]
+            src = raws[which][:].rearrange("p j (l t) -> p l j t", t=PACK)[:, l0:l1, :, LAST]
+            if on_scalar:
+                nc.scalar.activation(dst, src, ACT.Copy)
+            else:
+                nc.vector.tensor_copy(dst, src)
+
+        def quantise(name, source):
+            width = source.shape[1] // PACK
+            code = keep.tile([P, width], U32, name="code" + name, align_bytes=64)
+            plane = keep.tile([P, width], U8, name="plane" + name, align_bytes=64)
+            nc.vector.quantize_mx(out=code[:].bitcast(FP8X4), scales=plane[:], in_=source)
+            return code, plane
+
+        def quantise_tile(which, m):
+            code, plane = quantise("%d_%d" % (which, m), grouped[which][:, m * P * PACK : (m + 1) * P * PACK])
+            codes[which, m] = code[:]
+            planes[which, m] = plane[:]
+
+        for which in range(2):
+            round_chunk(which, 0)
+            quantise_tile(which, 0)
+
+        bias_seq = keep.tile([P, LAST * P], F32, name="bias_seq")
+        bias_lt = bias_row[:].rearrange("p (l t) -> p l t", t=PACK)
+        nc.scalar.activation(bias_seq[:].rearrange("p (l t) -> p l t", t=LAST), bias_lt[:, :, 0:LAST], ACT.Copy)
+        bias_t = acc_pool.tile([P, TILES, P], F32, name="bias_t", tag="acc")
+        for m in range(LAST):
+            nc.tensor.transpose(bias_t[:, m, :], bias_seq[:, m * P : (m + 1) * P], ident[:])
+        nc.tensor.transpose(bias_t[:, LAST, :], bias_lt[:, :, LAST], ident[:])
+        half_bias = keep.tile([P, TILES], F32, name="half_bias")
+        nc.scalar.activation(half_bias[:], bias_t[:, :, 0], ACT.Copy, scale=0.5)
+        for which in range(2):
+            round_last(which, 0, CHUNKS[0][1], True)
 
         half = I // 2
         quarter = I // 4
         node_plane = [keep.tile([P, half], U8, name="nplane%d" % h, align_bytes=64) for h in range(2)]
         node_code = [keep.tile([P, half], U32, name="ncode%d" % h, align_bytes=64) for h in range(2)]
-        quantise_weight(0, 0, round_weight(0, 0))
         for h in range(2):
             nc.vector.tensor_copy(node_plane[h][:], scale_pool[:].indirect(offsets[:, h * 32 : (h + 1) * 32]))
         for s in range(4):
@@ -106,103 +130,121 @@ def tile_attend_gatedreadout_pl_kernel(tc, node_words, node_scales, wg, wv, bg, 
                 node_code[s // 2][:, (s % 2) * quarter : (s % 2 + 1) * quarter],
                 word_pool[:].bitcast(U32).indirect(offsets[:, s * 16 : (s + 1) * 16]),
             )
-        quantise_weight(1, 0, round_weight(1, 0))
-        for s in (1, 2):
-            pair = [round_weight(which, s) for which in range(2)]
+        for chunk in (1, 2):
             for which in range(2):
-                quantise_weight(which, s, pair[which])
+                round_chunk(which, chunk)
+                if chunk == 2:
+                    round_last(which, CHUNKS[0][1], P, False)
+                quantise_tile(which, chunk)
+        code, plane = quantise("_last", grouped_last[:].rearrange("p w c -> p (w c)"))
+        for which in range(2):
+            codes[which, LAST] = code[:, which * P : (which + 1) * P]
+            planes[which, LAST] = plane[:, which * P : (which + 1) * P]
 
-        sums_a = sum_pool.tile([P, TILES - 1, P], F32, name="sums_a")
-        sums_b = sum_pool.tile([P, P], F32, name="sums_b")
+        sums = sum_pool.tile([P, LAST, P], F32, name="sums")
         acts = {}
 
-        def project(which, m, h, width):
-            acc = acc_pool.tile([P, BANK], F32, name="acc", tag="acc")
-            for c in range(0, BANK, width):
-                nc.tensor.matmul_mx(
-                    out=acc[:, c : c + width],
-                    lhsT=codes[which, m].bitcast(FP8X4),
-                    lhsT_scale=planes[which, m],
-                    rhs=node_code[h][:, c : c + width].bitcast(FP8X4),
-                    rhs_scale=node_plane[h][:, c : c + width],
-                    start=True,
-                    stop=True,
-                )
+        def project(which, m, s0, s1):
+            acc = acc_pool.tile([P, s1 - s0], F32, name="acc", tag="acc")
+            h, c0, c1 = s0 // half, s0 % half, s0 % half + s1 - s0
+            nc.tensor.matmul_mx(
+                out=acc[:],
+                lhsT=codes[which, m].bitcast(FP8X4),
+                lhsT_scale=planes[which, m],
+                rhs=node_code[h][:, c0:c1].bitcast(FP8X4),
+                rhs_scale=node_plane[h][:, c0:c1],
+                start=True,
+                stop=True,
+            )
             return acc
 
-        def activate(which, m, h, acc, g0, g1, j0, j1):
-            src = acc[:, g0 * J : g1 * J].rearrange("p (b i j) -> p b j i", i=4, j=J)[:, :, j0:j1, :]
-            dst = acts[which, m][:, j0:j1, 64 * h + g0 : 64 * h + g1].rearrange("p j (b i) -> p b j i", i=4)
+        def tanh(which, m, dst, src):
             if which == 0:
                 nc.scalar.activation(dst, src, ACT.Tanh, bias=half_bias[:, m : m + 1], scale=0.5)
             else:
                 nc.scalar.activation(dst, src, ACT.Tanh)
 
-        def gate(m, j0, j1):
-            tag = "late" if m == 0 else "prod%d_%d" % (m, j0)
-            prod = keep.tile([P, j1 - j0, P], F32, name="prod", tag=tag, align_bytes=64)
-            nc.vector.scalar_tensor_tensor(
-                prod[:], acts[0, m][:, j0:j1, :], 1.0, acts[1, m][:, j0:j1, :], ALU.add, ALU.mult
-            )
-            target = sums_b[:] if m == TILES - 1 else sums_a[:, m, :]
+        def activate(which, m, s0, s1):
+            src = project(which, m, s0, s1)[:].rearrange("p (b i j) -> p b j i", i=4, j=J)
+            dst = acts[which, m][:].rearrange("p (j g) -> p j g", j=J)[:, :, s0 // J : s1 // J]
+            tanh(which, m, dst.rearrange("p j (b i) -> p b j i", i=4), src)
+
+        def gate(m, prod, rows, cols):
+            views = [t[:].rearrange("p (r c) -> p r c", r=J)[:, rows, cols] for t in (prod, acts[0, m], acts[1, m])]
+            nc.vector.scalar_tensor_tensor(views[0], views[1], 1.0, views[2], ALU.add, ALU.mult)
+
+        def turn(m, prod, j0, j1):
             for j in range(j0, j1):
-                nc.tensor.matmul(target, prod[:, j - j0, :], ident[:], start=(j == 0), stop=(j == J - 1), is_transpose=True)
+                nc.tensor.matmul(
+                    sums[:, m, :], prod[:, j * P : (j + 1) * P], ident[:], start=(j == 0), stop=(j == J - 1), is_transpose=True
+                )
+
+        def gate_and_turn(m):
+            tag = "grouped1" if m == 0 else "prod%d" % m
+            prod = keep.tile([P, I], F32, name="prod", tag=tag, align_bytes=64)
+            if m < LAST - 1:
+                gate(m, prod, slice(0, J), slice(0, G))
+                turn(m, prod, 0, J)
+            else:
+                gate(m, prod, slice(0, J), slice(0, G // 2))
+                for j0 in (0, J // 2):
+                    gate(m, prod, slice(j0, j0 + J // 2), slice(G // 2, G))
+                    turn(m, prod, j0, j0 + J // 2)
 
         def front(m):
             for which in range(2):
-                acts[which, m] = work.tile([P, J, P], F32, name="act%d" % which, tag="act%d" % which, bufs=TILES)
-            if m == 0:
+                acts[which, m] = keep.tile([P, I], F32, name="act%d_%d" % (which, m))
+            step = quarter if m == 0 else half
+            for s0 in range(0, I, step):
                 for which in range(2):
-                    for h in range(2):
-                        acc = project(which, m, h, quarter)
-                        activate(which, m, h, acc, 0, 32, 0, J)
-                        activate(which, m, h, acc, 32, 64, 0, J)
-            elif m < TILES - 1:
-                for which in range(2):
-                    for h in range(2):
-                        activate(which, m, h, project(which, m, h, BANK), 0, 64, 0, J)
-            else:
-                for h in range(2):
-                    activate(0, m, h, project(0, m, h, BANK), 0, 64, 0, J)
-                accs = [project(1, m, h, BANK) for h in range(2)]
-                for j0, j1 in ((0, 4), (4, 6), (6, 8)):
-                    for h in range(2):
-                        activate(1, m, h, accs[h], 0, 64, j0, j1)
+                    activate(which, m, s0, s0 + step)
 
         front(0)
-        for m in range(1, TILES):
-            front(m)
-            gate(m - 1, 0, J)
-        by_graph = keep.tile([P, PACK, P], F32, name="by_graph")
-        nc.scalar.activation(
-            by_graph[:, :, 0:96].rearrange("g t (b i) -> g b t i", i=4),
-            sums_a[:].rearrange("g m (b i t) -> g (m b) t i", i=4, t=PACK),
-            ACT.Copy,
-            scale=0.5,
-        )
-        for j0, j1 in ((0, 4), (4, 6), (6, 8)):
-            gate(TILES - 1, j0, j1)
-        nc.scalar.activation(
-            by_graph[:, :, 96:128].rearrange("g t (b i) -> g b t i", i=4),
-            sums_b[:].rearrange("g (b i t) -> g b t i", i=4, t=PACK),
-            ACT.Copy,
-            scale=0.5,
-        )
+        front(1)
+        gate_and_turn(0)
+        front(2)
+        gate_and_turn(1)
 
-        result = acc_pool.tile([P, PACK, P], F32, name="result", tag="acc")
-        for t in range(PACK):
+        for which in range(2):
+            acts[which, LAST] = keep.tile([P, I], F32, name="act%d_%d" % (which, LAST))
+        for h in range(2):
+            tanh(0, LAST, acts[0, LAST][:, h * half : (h + 1) * half], project(0, LAST, h * half, (h + 1) * half)[:])
+            acc = project(1, LAST, h * half, (h + 1) * half)
+            step = half if h == 0 else quarter
+            for c in range(0, half, step):
+                tanh(1, LAST, acts[1, LAST][:, h * half + c : h * half + c + step], acc[:, c : c + step])
+        gate_and_turn(2)
+
+        twice = keep.tile([P, PACK, G], F32, name="twice")
+        by_graph = keep.tile([P, LAST, P], F32, name="by_graph")
+        nc.scalar.activation(
+            by_graph[:].rearrange("g t l -> g l t"), sums[:].rearrange("g m c -> g (m c)").rearrange("g (l t) -> g l t", t=LAST), ACT.Copy
+        )
+        result = acc_pool.tile([P, LAST, P], F32, name="result", tag="acc")
+        for t in range(LAST):
             nc.tensor.transpose(result[:, t, :], by_graph[:, t, :], ident[:])
-        result2 = acc_pool.tile([P, PACK, P], F32, name="result2", tag="acc")
-        for t in range(PACK):
-            nc.tensor.transpose(result2[:, t, :], by_graph[:, t, :], ident[:])
+        nc.scalar.activation(twice[:, 0:LAST, :], result[:], ACT.Copy)
+        y_rows = keep.tile([P, PACK, G], F32, name="y_rows")
+        nc.scalar.activation(y_rows[:, 0:LAST, :], result[:], ACT.Copy, scale=0.5)
+
+        prod = keep.tile([P, I], F32, name="prod_last")
+        pieces = ((0, half), (half, half + quarter), (half + quarter, I))
+        for c0, c1 in pieces:
+            gate(LAST, prod, slice(c0 // P, c1 // P), slice(0, P))
+            nc.vector.tensor_reduce(
+                twice[:, LAST, c0 // J : c1 // J], prod[:, c0:c1].rearrange("p (g j) -> p g j", j=J), AXIS.X, ALU.add
+            )
+        nc.scalar.activation(y_rows[:, LAST, :], twice[:, LAST, :], ACT.Copy, scale=0.5)
 
         rounded = keep.tile([P, G * PACK], BF16, name="rounded", align_bytes=64)
-        nc.vector.tensor_copy(rounded[:].rearrange("p (g t) -> p g t", t=PACK), result[:].rearrange("p t g -> p g t"))
-        y_code = keep.tile([P, G], U32, name="y_code", align_bytes=64)
-        y_plane = keep.tile([P, G], U8, name="y_plane", align_bytes=64)
-        nc.vector.quantize_mx(out=y_code[:].bitcast(FP8X4), scales=y_plane[:], in_=rounded[:])
-        y_rows = keep.tile([P, PACK, G], F32, name="y_rows")
-        nc.scalar.copy(y_rows[:], result2[:])
+        nc.vector.tensor_scalar(
+            rounded[:].rearrange("p (c i t) -> p c t i", i=4, t=PACK),
+            twice[:].rearrange("p t (c i) -> p c t i", i=4),
+            0.5,
+            None,
+            ALU.mult,
+        )
+        y_code, y_plane = quantise("_y", rounded[:])
         nc.scalar.dma_start(out_0.rearrange("(p t) g -> p t g", t=PACK), y_rows[:])
         nc.sync.dma_start(out_1[0].rearrange("p g t -> p (g t)").bitcast(I32), y_code[:].bitcast(I32))
         for q in range(4):

from contextlib import ExitStack

import concourse.mybir as mybir
from concourse.masks import make_identity

K, T, I, G, E = 512, 2048, 1024, 128, 512
FLOPS = 2 * 2 * K * E * I

F32 = mybir.dt.float32
BF16 = mybir.dt.bfloat16
I32 = mybir.dt.int32
U32 = mybir.dt.uint32
U16 = mybir.dt.uint16
U8 = mybir.dt.uint8
FP8X4 = mybir.dt.float8_e4m3fn_x4
ACT = mybir.ActivationFunctionType
ALU = mybir.AluOpType
AXIS = mybir.AxisListType

P = 128
PACK = 4
J = I // G
TILES = E // P
LAST = TILES - 1
CHUNKS = ((0, 44), (44, 88), (88, 128))


def tile_attend_gatedreadout_pl_kernel(tc, node_words, node_scales, wg, wv, bg, offs, out_0, out_1, out_2):
    nc = tc.nc
    with ExitStack() as ctx:
        keep = ctx.enter_context(tc.tile_pool(name="keep", bufs=1))
        acc_pool = ctx.enter_context(tc.psum_pool(name="acc", bufs=7))
        sum_pool = ctx.enter_context(tc.psum_pool(name="sums", bufs=1))

        offsets = keep.tile([P, I // 16], U16, name="offsets")
        nc.sync.dma_start(offsets[:], offs)

        weights = (wg, wv)
        raws = [keep.tile([P, PACK, E], F32, name="raw%d" % which) for which in range(2)]

        def load_weight(which, chunk):
            c0, c1 = CHUNKS[chunk][0] * PACK, CHUNKS[chunk][1] * PACK
            nc.sync.dma_start(
                raws[which][:, :, c0:c1], weights[which][:, c0:c1].rearrange("(p j) c -> p j c", j=PACK)
            )

        scale_pool = keep.tile([P, T], U8, name="scale_pool", align_bytes=64)
        nc.vector.memset(scale_pool[:].bitcast(I32), 0)
        bias_row = keep.tile([P, E], F32, name="bias_row")
        nc.gpsimd.memset(bias_row[:], 0.0)
        ident = keep.tile([P, P], F32, name="ident")
        make_identity(nc, ident[:])

        load_weight(0, 0)
        for q in range(4):
            engine = nc.sync if q < 2 else nc.scalar
            engine.dma_start(
                scale_pool[32 * q : 32 * q + 4, :].bitcast(I32),
                node_scales[0, 4 * q : 4 * q + 4, :].bitcast(I32),
            )
        load_weight(1, 0)
        nc.sync.dma_start(bias_row[0:1, :], bg.rearrange("e o -> o e"))
        word_pool = keep.tile([P, T], I32, name="word_pool", align_bytes=64)
        nc.sync.dma_start(word_pool[:], node_words[0].rearrange("p n t -> p (n t)").bitcast(I32))
        for chunk in (1, 2):
            for which in range(2):
                load_weight(which, chunk)

        grouped = [
            keep.tile([P, LAST * P * PACK], BF16, name="grouped", tag="grouped%d" % which, align_bytes=64)
            for which in range(2)
        ]
        grouped_last = keep.tile([P, 2, P * PACK], BF16, name="grouped_last", align_bytes=64)
        codes = {}
        planes = {}

        def round_chunk(which, chunk):
            l0, l1 = CHUNKS[chunk]
            dst = grouped[which][:].rearrange("p (l t j) -> p l j t", t=LAST, j=PACK)[:, l0:l1, :, :]
            src = raws[which][:].rearrange("p j (l t) -> p l j t", t=PACK)[:, l0:l1, :, 0:LAST]
            if chunk == 0:
                nc.scalar.activation(dst, src, ACT.Copy)
            else:
                nc.vector.tensor_copy(dst, src)

        def round_last(which, l0, l1, on_scalar):
            dst = grouped_last[:, which, :].rearrange("p (l j) -> p l j", j=PACK)[:, l0:l1, :]
            src = raws[which][:].rearrange("p j (l t) -> p l j t", t=PACK)[:, l0:l1, :, LAST]
            if on_scalar:
                nc.scalar.activation(dst, src, ACT.Copy)
            else:
                nc.vector.tensor_copy(dst, src)

        def quantise(name, source):
            width = source.shape[1] // PACK
            code = keep.tile([P, width], U32, name="code" + name, align_bytes=64)
            plane = keep.tile([P, width], U8, name="plane" + name, align_bytes=64)
            nc.vector.quantize_mx(out=code[:].bitcast(FP8X4), scales=plane[:], in_=source)
            return code, plane

        def quantise_tile(which, m):
            code, plane = quantise("%d_%d" % (which, m), grouped[which][:, m * P * PACK : (m + 1) * P * PACK])
            codes[which, m] = code[:]
            planes[which, m] = plane[:]

        for which in range(2):
            round_chunk(which, 0)
            quantise_tile(which, 0)

        bias_seq = keep.tile([P, LAST * P], F32, name="bias_seq")
        bias_lt = bias_row[:].rearrange("p (l t) -> p l t", t=PACK)
        nc.scalar.activation(bias_seq[:].rearrange("p (l t) -> p l t", t=LAST), bias_lt[:, :, 0:LAST], ACT.Copy)
        bias_t = acc_pool.tile([P, TILES, P], F32, name="bias_t", tag="acc")
        for m in range(LAST):
            nc.tensor.transpose(bias_t[:, m, :], bias_seq[:, m * P : (m + 1) * P], ident[:])
        nc.tensor.transpose(bias_t[:, LAST, :], bias_lt[:, :, LAST], ident[:])
        half_bias = keep.tile([P, TILES], F32, name="half_bias")
        nc.scalar.activation(half_bias[:], bias_t[:, :, 0], ACT.Copy, scale=0.5)
        for which in range(2):
            round_last(which, 0, CHUNKS[0][1], True)

        half = I // 2
        quarter = I // 4
        node_plane = [keep.tile([P, half], U8, name="nplane%d" % h, align_bytes=64) for h in range(2)]
        node_code = [keep.tile([P, half], U32, name="ncode%d" % h, align_bytes=64) for h in range(2)]
        for h in range(2):
            nc.vector.tensor_copy(node_plane[h][:], scale_pool[:].indirect(offsets[:, h * 32 : (h + 1) * 32]))
        for s in range(4):
            nc.vector.tensor_copy(
                node_code[s // 2][:, (s % 2) * quarter : (s % 2 + 1) * quarter],
                word_pool[:].bitcast(U32).indirect(offsets[:, s * 16 : (s + 1) * 16]),
            )
        for chunk in (1, 2):
            for which in range(2):
                round_chunk(which, chunk)
                if chunk == 2:
                    round_last(which, CHUNKS[0][1], P, False)
                quantise_tile(which, chunk)
        code, plane = quantise("_last", grouped_last[:].rearrange("p w c -> p (w c)"))
        for which in range(2):
            codes[which, LAST] = code[:, which * P : (which + 1) * P]
            planes[which, LAST] = plane[:, which * P : (which + 1) * P]

        sums = sum_pool.tile([P, LAST, P], F32, name="sums")
        acts = {}

        def project(which, m, s0, s1):
            acc = acc_pool.tile([P, s1 - s0], F32, name="acc", tag="acc")
            h, c0, c1 = s0 // half, s0 % half, s0 % half + s1 - s0
            nc.tensor.matmul_mx(
                out=acc[:],
                lhsT=codes[which, m].bitcast(FP8X4),
                lhsT_scale=planes[which, m],
                rhs=node_code[h][:, c0:c1].bitcast(FP8X4),
                rhs_scale=node_plane[h][:, c0:c1],
                start=True,
                stop=True,
            )
            return acc

        def tanh(which, m, dst, src):
            if which == 0:
                nc.scalar.activation(dst, src, ACT.Tanh, bias=half_bias[:, m : m + 1], scale=0.5)
            else:
                nc.scalar.activation(dst, src, ACT.Tanh)

        def activate(which, m, s0, s1):
            src = project(which, m, s0, s1)[:].rearrange("p (b i j) -> p b j i", i=4, j=J)
            dst = acts[which, m][:].rearrange("p (j g) -> p j g", j=J)[:, :, s0 // J : s1 // J]
            tanh(which, m, dst.rearrange("p j (b i) -> p b j i", i=4), src)

        def gate(m, prod, rows, cols):
            views = [t[:].rearrange("p (r c) -> p r c", r=J)[:, rows, cols] for t in (prod, acts[0, m], acts[1, m])]
            nc.vector.scalar_tensor_tensor(views[0], views[1], 1.0, views[2], ALU.add, ALU.mult)

        def turn(m, prod, j0, j1):
            for j in range(j0, j1):
                nc.tensor.matmul(
                    sums[:, m, :], prod[:, j * P : (j + 1) * P], ident[:], start=(j == 0), stop=(j == J - 1), is_transpose=True
                )

        def gate_and_turn(m):
            tag = "grouped1" if m == 0 else "prod%d" % m
            prod = keep.tile([P, I], F32, name="prod", tag=tag, align_bytes=64)
            if m < LAST - 1:
                gate(m, prod, slice(0, J), slice(0, G))
                turn(m, prod, 0, J)
            else:
                gate(m, prod, slice(0, J), slice(0, G // 2))
                for j0 in (0, J // 2):
                    gate(m, prod, slice(j0, j0 + J // 2), slice(G // 2, G))
                    turn(m, prod, j0, j0 + J // 2)

        def front(m):
            for which in range(2):
                acts[which, m] = keep.tile([P, I], F32, name="act%d_%d" % (which, m))
            step = quarter if m == 0 else half
            for s0 in range(0, I, step):
                for which in range(2):
                    activate(which, m, s0, s0 + step)

        front(0)
        front(1)
        gate_and_turn(0)
        front(2)
        gate_and_turn(1)

        for which in range(2):
            acts[which, LAST] = keep.tile([P, I], F32, name="act%d_%d" % (which, LAST))
        for h in range(2):
            tanh(0, LAST, acts[0, LAST][:, h * half : (h + 1) * half], project(0, LAST, h * half, (h + 1) * half)[:])
            acc = project(1, LAST, h * half, (h + 1) * half)
            step = half if h == 0 else quarter
            for c in range(0, half, step):
                tanh(1, LAST, acts[1, LAST][:, h * half + c : h * half + c + step], acc[:, c : c + step])
        gate_and_turn(2)

        twice = keep.tile([P, PACK, G], F32, name="twice")
        by_graph = keep.tile([P, LAST, P], F32, name="by_graph")
        nc.scalar.activation(
            by_graph[:].rearrange("g t l -> g l t"), sums[:].rearrange("g m c -> g (m c)").rearrange("g (l t) -> g l t", t=LAST), ACT.Copy
        )
        result = acc_pool.tile([P, LAST, P], F32, name="result", tag="acc")
        for t in range(LAST):
            nc.tensor.transpose(result[:, t, :], by_graph[:, t, :], ident[:])
        nc.scalar.activation(twice[:, 0:LAST, :], result[:], ACT.Copy)
        y_rows = keep.tile([P, PACK, G], F32, name="y_rows")
        nc.scalar.activation(y_rows[:, 0:LAST, :], result[:], ACT.Copy, scale=0.5)

        prod = keep.tile([P, I], F32, name="prod_last")
        pieces = ((0, half), (half, half + quarter), (half + quarter, I))
        for c0, c1 in pieces:
            gate(LAST, prod, slice(c0 // P, c1 // P), slice(0, P))
            nc.vector.tensor_reduce(
                twice[:, LAST, c0 // J : c1 // J], prod[:, c0:c1].rearrange("p (g j) -> p g j", j=J), AXIS.X, ALU.add
            )
        nc.scalar.activation(y_rows[:, LAST, :], twice[:, LAST, :], ACT.Copy, scale=0.5)

        rounded = keep.tile([P, G * PACK], BF16, name="rounded", align_bytes=64)
        nc.vector.tensor_scalar(
            rounded[:].rearrange("p (c i t) -> p c t i", i=4, t=PACK),
            twice[:].rearrange("p t (c i) -> p c t i", i=4),
            0.5,
            None,
            ALU.mult,
        )
        y_code, y_plane = quantise("_y", rounded[:])
        nc.scalar.dma_start(out_0.rearrange("(p t) g -> p t g", t=PACK), y_rows[:])
        nc.sync.dma_start(out_1[0].rearrange("p g t -> p (g t)").bitcast(I32), y_code[:].bitcast(I32))
        for q in range(4):
            engine = nc.sync if q % 2 == 0 else nc.scalar
            engine.dma_start(
                out_2[0, 4 * q : 4 * q + 4, :].bitcast(I32), y_plane[32 * q : 32 * q + 4, :].bitcast(I32)
            )
